import numpy as np
import ml_dtypes


def mxq(x, axis, fmt="e4m3"):
    dtype, down = {"e4m3": (ml_dtypes.float8_e4m3fn, 7), "e5m2": (ml_dtypes.float8_e5m2, 14)}[fmt]
    v = np.moveaxis(np.asarray(x, np.float32).astype(ml_dtypes.bfloat16).astype(np.float64), axis, -1)
    blocks = v.reshape(v.shape[:-1] + (-1, 32))
    amax = np.abs(blocks).max(-1, keepdims=True)
    byte = np.maximum(np.where(amax > 0, np.frexp(amax)[1] - 1 + 127, 0) - down, 1)
    scale = np.exp2(byte - 127.0)
    codes = (blocks / scale).astype(np.float32).astype(dtype).astype(np.float64)
    return np.moveaxis((codes * scale).reshape(v.shape), -1, axis)


WIDE = False


def mx_kscale(k):
    if not WIDE:
        return np.ones(k)
    levels = np.array([10, -10, 5, -5, 0])
    if k % 512:
        return np.exp2(np.random.permutation(np.resize(levels, k // 32))).repeat(32)
    a = np.empty((k // 512, 16))
    for p in range(k // 512):
        a[p, :8] = np.random.permutation(np.resize(levels, 8))
        for g in range(8):
            far = levels[np.abs(levels - a[p, g]) >= 10]
            a[p, g + 8] = far[np.random.randint(len(far))]
    return np.exp2(a.ravel()).repeat(32)


BF16 = ml_dtypes.bfloat16


def bf(x):
    return np.asarray(x, np.float32).astype(BF16)


def f64(x):
    return np.asarray(x).astype(np.float64)


E2M1 = np.array([0.0, 0.5, 1.0, 1.5, 2.0, 3.0, 4.0, 6.0, -0.0, -0.5, -1.0, -1.5, -2.0, -3.0, -4.0, -6.0])


def pack_weight(w, fmt):
    k, n = w.shape
    w = f64(bf(w)).reshape(k // 32, 32, n)
    amax = np.abs(w).max(1)
    if fmt == "e4m3":
        byte = np.frexp(amax)[1] - 1 + 127 - 7
    else:
        mant, ex = np.frexp(amax / 6.0)
        byte = np.where(mant > 0.5, ex, ex - 1) + 127
    byte = np.clip(np.where(amax > 0, byte, 1), 1, 254)
    scaled = (w * np.exp2(127.0 - byte)[:, None, :]).reshape(k, n).astype(np.float32)
    by_word = np.ascontiguousarray(scaled.reshape(k // 512, 128, 4, n).transpose(0, 1, 3, 2))
    if fmt == "e4m3":
        words = by_word.astype(ml_dtypes.float8_e4m3fn).view(np.uint8)
    else:
        c = by_word.astype(ml_dtypes.float4_e2m1fn).view(np.uint8) & 0xF
        words = c[..., 0::2] | (c[..., 1::2] << 4)
    return np.ascontiguousarray(words), np.ascontiguousarray(byte.astype(np.uint8).reshape(k // 512, 16, n))


def unpack_weight(words, scales, fmt):
    g, p, n, _ = words.shape
    if fmt == "e4m3":
        vals = np.ascontiguousarray(words).view(ml_dtypes.float8_e4m3fn).astype(np.float64)
    else:
        nib = np.empty((g, p, n, 4), np.uint8)
        nib[..., 0::2] = words & 0xF
        nib[..., 1::2] = words >> 4
        vals = E2M1[nib]
    vals = vals * np.repeat(np.exp2(scales.astype(np.float64) - 127.0), 8, axis=1)[..., None]
    return vals.transpose(0, 1, 3, 2).reshape(g * 512, n)
def pack4(w):
    words, scales = pack_weight(w, "e2m1")
    return words.reshape(words.shape[0], 128, -1), scales


def unpack4(words, scales):
    return unpack_weight(words.reshape(words.shape[0], 128, -1, 2), scales, "e2m1")


def planes(Y):
    n, m = Y.shape
    b = f64(bf(Y)).reshape(n // 32, 32, m)
    amax = np.abs(b).max(1)
    byte = np.clip(np.where(amax > 0, np.frexp(amax)[1] - 1 + 127 - 7, 1), 1, 254)
    codes = (b * np.exp2(127.0 - byte)[:, None, :]).reshape(n, m).astype(np.float32).astype(ml_dtypes.float8_e4m3fn).view(np.uint8)
    words = codes.reshape(n // 512, 128, 4, m).transpose(0, 1, 3, 2)
    return np.ascontiguousarray(words), np.ascontiguousarray(byte.astype(np.uint8).reshape(n // 512, 16, m))


B, T, C, D = 4, 256, 1024, 2048

def setup_inputs():
    s = mx_kscale(C)
    x = np.random.randn(B, T, C) * s
    spread = np.exp(0.8 * np.random.randn(D))
    wv = np.random.randn(C, D) / np.sqrt(C) * spread / s[:, None]
    wg = 1.5 * np.random.randn(C, D) / np.sqrt(C) / s[:, None]
    wv_words, wv_scales = pack4(wv)
    wg_words, wg_scales = pack4(wg)
    return {
        "x": bf(x),
        "wv_words": wv_words,
        "wv_scales": wv_scales,
        "wg_words": wg_words,
        "wg_scales": wg_scales,
        "value_bias": bf(0.4 * np.random.randn(D) * spread),
        "gate_bias": bf(0.5 * np.random.randn(D)),
    }

def reference(x, wv_words, wv_scales, wg_words, wg_scales, value_bias, gate_bias):
    xq = mxq(f64(x).reshape(B * T, C), 1, "e4m3")
    wv = unpack4(wv_words, wv_scales)
    wg = unpack4(wg_words, wg_scales)
    value = (xq @ wv) + f64(value_bias)
    gate = (xq @ wg) + f64(gate_bias)
    y = (value * (1.0 / (1.0 + np.exp(-gate)))).reshape(B, T, D)
    Y = y.reshape(B * T, D).T
    words, scales = planes(Y)
    return y, words, scales

@@ -1,0 +1,319 @@
+from contextlib import ExitStack
+
+import concourse.mybir as mybir
+from concourse.masks import make_identity
+
+F32 = mybir.dt.float32
+BF16 = mybir.dt.bfloat16
+I32 = mybir.dt.int32
+U32 = mybir.dt.uint32
+U8 = mybir.dt.uint8
+FP8X4 = mybir.dt.float8_e4m3fn_x4
+FP4X4 = mybir.dt.float4_e2m1fn_x4
+ACT = mybir.ActivationFunctionType
+ALU = mybir.AluOpType
+
+TOKENS, C, D = 1024, 1024, 2048
+FLOPS = 2 * 2 * TOKENS * C * D
+
+P = 128
+PACK = 4
+SPAN = P * PACK
+PASSES = C // SPAN
+GROUPS = D // SPAN
+HALF = 512
+HALVES = TOKENS // HALF
+BLOCKS = HALF // P
+UNITS = GROUPS * HALVES
+GATE, VALUE = 0, 1
+CAST_SPLIT = 384
+
+
+def tile_conformer_pointwise_glu_g4_kernel(
+    tc, x, wv_words, wv_scales, wg_words, wg_scales, value_bias, gate_bias, out_0, out_1, out_2
+):
+    nc = tc.nc
+    x_rows = x.rearrange("b f c -> (b f) c")
+    y_rows = out_0.rearrange("b f d -> (b f) d")
+    words_in = {GATE: wg_words, VALUE: wv_words}
+    scales_in = {GATE: wg_scales, VALUE: wv_scales}
+    bias_in = {GATE: gate_bias, VALUE: value_bias}
+
+    with ExitStack() as ctx:
+        keep = ctx.enter_context(tc.tile_pool(name="keep", bufs=1))
+        work = ctx.enter_context(tc.tile_pool(name="work", bufs=2))
+        psum = ctx.enter_context(tc.psum_pool(name="psum", bufs=2))
+        ctx.enter_context(tc.manual_schedule())
+
+        ident = keep.tile([P, P], F32, name="ident")
+        warm_in = keep.tile([P, 8], F32, name="warm_in")
+        warm_out = keep.tile([P, 8], F32, name="warm_out")
+        x_first = [keep.tile([P, C], BF16, name="x_first%d" % b) for b in range(BLOCKS)]
+        x_split = [keep.tile([P, C // 2], F32, name="x_split%d" % b) for b in range(BLOCKS)]
+        x_second = keep.tile([P, BLOCKS, C], BF16, name="x_second")
+        x_grouped = [
+            keep.tile([P, PASSES, HALF * PACK], BF16, name="x_grouped%d" % h, align_bytes=64) for h in range(HALVES)
+        ]
+        x_codes = [keep.tile([P, PASSES, HALF], U32, name="x_codes%d" % h, align_bytes=64) for h in range(HALVES)]
+        x_scales = [keep.tile([P, PASSES, HALF], U8, name="x_scales%d" % h, align_bytes=64) for h in range(HALVES)]
+        raw_words = [keep.tile([P, 2, PASSES, 2 * SPAN], U8, name="raw_words%d" % g) for g in range(GROUPS)]
+        raw_scales_first = keep.tile([P, 2, PASSES, SPAN], U8, name="raw_scales_first")
+        raw_scales_rest = keep.tile([P, 2, PASSES, D - SPAN], U8, name="raw_scales_rest")
+        w_words = [
+            keep.tile([P, PACK, 2, PASSES, 2 * P], U8, name="w_words%d" % g, align_bytes=64) for g in range(GROUPS)
+        ]
+        w_scales = [
+            keep.tile([P, 2, PACK, PASSES, P], U8, name="w_scales%d" % g, align_bytes=64) for g in range(GROUPS)
+        ]
+        bias = [keep.tile([P, GROUPS, PACK], BF16, name="bias%d" % w) for w in range(2)]
+        y_scales_early = keep.tile([P, GROUPS - 1, TOKENS], U8, name="y_scales_early", align_bytes=64)
+        y_scales_last = keep.tile([P, 1, TOKENS], U8, name="y_scales_last", align_bytes=64)
+
+        live = {}
+
+        def load_scales(queue, tile, w, cols):
+            for q in range(4):
+                queue.dma_start(
+                    out=tile[32 * q : 32 * q + 4, w].bitcast(I32),
+                    in_=scales_in[w][:, 4 * q : 4 * q + 4, cols].rearrange("k r n -> r k n").bitcast(I32),
+                )
+
+        def load_words(g, w):
+            nc.sync.dma_start(
+                out=raw_words[g][:, w].bitcast(I32),
+                in_=words_in[w][:, :, 2 * SPAN * g : 2 * SPAN * (g + 1)].rearrange("k p n -> p k n").bitcast(I32),
+            )
+
+        def split_x(b):
+            nc.vector.tensor_copy(
+                out=x_split[b][:].rearrange("r (k u p) -> r k u p", k=PASSES, u=2),
+                in_=x_first[b][:].bitcast(F32).rearrange("r (k p u) -> r k u p", k=PASSES, u=2),
+            )
+
+        def turn_x(h, b):
+            bank = psum.tile([P, PASSES, 2, P], F32, name="turn", tag="turn", bufs=4)
+            live["x", h, b] = bank
+            for k in range(PASSES):
+                for u in range(2):
+                    if h == 0:
+                        src = x_split[b][:, (2 * k + u) * P : (2 * k + u + 1) * P]
+                    else:
+                        src = x_second[:, b, :].bitcast(F32)[:, 2 * P * k + u : 2 * P * (k + 1) : 2]
+                    nc.tensor.transpose(bank[:, k, u, :], src, ident[:])
+
+        def group_x(h, b):
+            nc.scalar.copy(
+                out=x_grouped[h][:, :, SPAN * b : SPAN * (b + 1)].bitcast(F32).rearrange("p k (r u) -> p k r u", u=2),
+                in_=live["x", h, b][:].rearrange("p k u r -> p k r u"),
+            )
+
+        def quantise_x(h, k, lo, hi):
+            nc.vector.quantize_mx(
+                out=x_codes[h][:, k, lo:hi].bitcast(FP8X4),
+                scales=x_scales[h][:, k, lo:hi],
+                in_=x_grouped[h][:, k, PACK * lo : PACK * hi],
+            )
+
+        def order_words(g, t, ws):
+            nc.vector.tensor_copy(
+                out=w_words[g][:, t, ws].rearrange("p w k (m e) -> p (w k m) e", e=2),
+                in_=raw_words[g][:, ws].rearrange("p w k (m t e) -> p t (w k m) e", t=PACK, e=2)[:, t],
+            )
+
+        def order_scales(g, w):
+            if g == 0:
+                src = raw_scales_first[:, w]
+            else:
+                src = raw_scales_rest[:, w, :, SPAN * (g - 1) : SPAN * g]
+            nc.vector.tensor_copy(out=w_scales[g][:, w], in_=src.rearrange("p k (m t) -> p t k m", t=PACK))
+
+        def multiply(n, t):
+            g, h = divmod(n, HALVES)
+            for w in (GATE, VALUE):
+                acc = psum.tile([P, HALF], F32, name="acc%d" % w, tag="acc%d" % w, bufs=2)
+                live["acc", w, n, t] = acc
+                for k in range(PASSES):
+                    nc.tensor.matmul_mx(
+                        out=acc[:],
+                        lhsT=w_words[g][:, t, w, k, :].bitcast(FP4X4),
+                        lhsT_scale=w_scales[g][:, w, t, k, :],
+                        rhs=x_codes[h][:, k, :].bitcast(FP8X4),
+                        rhs_scale=x_scales[h][:, k, :],
+                        start=(k == 0),
+                        stop=(k == PASSES - 1),
+                    )
+
+        def sigmoid(n, t):
+            g = n // HALVES
+            sig = work.tile([P, HALF], F32, name="sig", tag="sig", bufs=3)
+            live["sig", n, t] = sig
+            nc.scalar.activation(
+                out=sig[:], in_=live["acc", GATE, n, t][:], func=ACT.Sigmoid, bias=bias[GATE][:, g, t : t + 1]
+            )
+
+        def product(n, t):
+            g = n // HALVES
+            if t == 0:
+                live["yt", n] = work.tile([P, PACK, HALF], F32, name="yt", tag="yt", bufs=2)
+            nc.vector.scalar_tensor_tensor(
+                out=live["yt", n][:, t, :],
+                in0=live["acc", VALUE, n, t][:],
+                scalar=bias[VALUE][:, g, t : t + 1],
+                in1=live["sig", n, t][:],
+                op0=ALU.add,
+                op1=ALU.mult,
+            )
+
+        def step(n, t):
+            multiply(n, t)
+            sigmoid(n, t)
+
+        def turn_y(n, order):
+            for b in range(BLOCKS):
+                live["turn", n, b] = psum.tile([P, PACK, P], F32, name="turn", tag="turn", bufs=4)
+            for b, t in order:
+                nc.tensor.transpose(
+                    live["turn", n, b][:, t, :], live["yt", n][:, t, P * b : P * (b + 1)], ident[:]
+                )
+
+        def copy_y(n, b):
+            if b == 0:
+                live["y", n] = work.tile([P, BLOCKS, SPAN], F32, name="y", tag="y", bufs=3)
+            nc.scalar.copy(
+                out=live["y", n][:, b, :].rearrange("r (p t) -> r p t", t=PACK),
+                in_=live["turn", n, b][:].rearrange("r t p -> r p t"),
+            )
+
+        def store_y(n, lo, hi):
+            g, h = divmod(n, HALVES)
+            rows = y_rows[HALF * h + P * lo : HALF * h + P * hi, SPAN * g : SPAN * (g + 1)]
+            nc.sync.dma_start(out=rows.rearrange("(b r) d -> r b d", r=P), in_=live["y", n][:, lo:hi, :])
+
+        def round_y(n, lo, hi, copy):
+            if ("yb", n) not in live:
+                live["yb", n] = work.tile([P, HALF * PACK], BF16, name="yb", tag="yb", bufs=2, align_bytes=64)
+            copy(
+                out=live["yb", n][:, PACK * lo : PACK * hi].rearrange("p (c i t) -> p c t i", i=4, t=PACK),
+                in_=live["yt", n][:, :, lo:hi].rearrange("p t (c i) -> p c t i", i=4),
+            )
+
+        def quantise_y(n):
+            g, h = divmod(n, HALVES)
+            codes = work.tile([P, HALF], U32, name="y_codes", tag="y_codes", bufs=3, align_bytes=64)
+            plane = y_scales_early[:, g] if g < GROUPS - 1 else y_scales_last[:, 0]
+            nc.vector.quantize_mx(
+                out=codes[:].bitcast(FP8X4), scales=plane[:, HALF * h : HALF * (h + 1)], in_=live["yb", n][:]
+            )
+            nc.sync.dma_start(
+                out=out_1[g, :, HALF * h : HALF * (h + 1), :].rearrange("p m t -> p (m t)").bitcast(I32),
+                in_=codes[:].bitcast(I32),
+            )
+
+        def store_scales(tile, lo, hi):
+            for q in range(4):
+                nc.sync.dma_start(
+                    out=out_2[lo:hi, 4 * q : 4 * q + 4, :].rearrange("g r m -> r g m").bitcast(I32),
+                    in_=tile[32 * q : 32 * q + 4].bitcast(I32),
+                )
+
+        both = slice(0, 2)
+
+        nc.vector.memset(raw_scales_first[:].rearrange("p w k n -> p (w k n)").bitcast(I32), 0)
+        nc.vector.memset(warm_in[:], 0.0)
+        make_identity(nc, ident[:])
+        load_scales(nc.scalar, raw_scales_first, GATE, slice(0, SPAN))
+        nc.scalar.activation(out=warm_out[:], in_=warm_in[:], func=ACT.Sigmoid)
+        nc.vector.memset(raw_scales_rest[:].rearrange("p w k n -> p (w k n)").bitcast(I32), 0)
+        for b in range(BLOCKS):
+            nc.sync.dma_start(out=x_first[b][:], in_=x_rows[P * b : P * (b + 1), :])
+        load_words(0, GATE)
+        load_words(0, VALUE)
+        load_scales(nc.sync, raw_scales_first, VALUE, slice(0, SPAN))
+        for w in (GATE, VALUE):
+            nc.sync.dma_start(out=bias[w][:], in_=bias_in[w].rearrange("(g p t) -> p g t", p=P, t=PACK))
+        nc.sync.dma_start(out=x_second[:], in_=x_rows[HALF:, :].rearrange("(b r) c -> r b c", r=P))
+        for w in (GATE, VALUE):
+            load_scales(nc.sync, raw_scales_rest, w, slice(SPAN, D))
+        for g in range(1, GROUPS):
+            load_words(g, GATE)
+            load_words(g, VALUE)
+
+        for b in range(BLOCKS):
+            split_x(b)
+            if b == 1:
+                order_scales(0, GATE)
+            turn_x(0, b)
+            group_x(0, b)
+        for b in range(BLOCKS - 1):
+            for k in range(PASSES):
+                quantise_x(0, k, P * b, P * (b + 1))
+        order_words(0, 0, slice(GATE, GATE + 1))
+        for k in range(PASSES):
+            quantise_x(0, k, P * (BLOCKS - 1), HALF)
+        order_words(0, 0, slice(VALUE, VALUE + 1))
+        order_scales(0, VALUE)
+
+        step(0, 0)
+        order_words(0, 1, both)
+        step(0, 1)
+        product(0, 0)
+        order_words(0, 2, both)
+        for b in range(BLOCKS):
+            turn_x(1, b)
+        group_x(1, 0)
+        group_x(1, 1)
+        product(0, 1)
+        order_words(0, 3, both)
+        step(0, 2)
+        group_x(1, 2)
+        group_x(1, 3)
+        step(0, 3)
+        product(0, 2)
+        for k in range(PASSES):
+            quantise_x(1, k, 0, HALF)
+
+        block_major = [(b, t) for b in range(BLOCKS) for t in range(PACK)]
+        for n in range(1, UNITS):
+            g, h = divmod(n, HALVES)
+            if h == 0:
+                chores = [lambda t=t, g=g: order_words(g, t, both) for t in (1, 2, 3)]
+            elif g + 1 < GROUPS:
+                chores = [
+                    lambda g=g: order_scales(g + 1, GATE),
+                    lambda g=g: order_scales(g + 1, VALUE),
+                    lambda g=g: order_words(g + 1, 0, both),
+                ]
+            else:
+                chores = [lambda: None] * 3
+            product(n - 1, 3)
+            step(n, 0)
+            chores[0]()
+            round_y(n - 1, CAST_SPLIT, HALF, nc.scalar.copy)
+            turn_y(n - 1, block_major)
+            product(n, 0)
+            chores[1]()
+            round_y(n - 1, 0, CAST_SPLIT, nc.vector.tensor_copy)
+            chores[2]()
+            for b in range(3):
+                copy_y(n - 1, b)
+            step(n, 1)
+            copy_y(n - 1, 3)
+            store_y(n - 1, 0, BLOCKS)
+            product(n, 1)
+            quantise_y(n - 1)
+            if n == UNITS - 2:
+                store_scales(y_scales_early, 0, GROUPS - 1)
+            step(n, 2)
+            product(n, 2)
+            step(n, 3)
+
+        n = UNITS - 1
+        product(n, 3)
+        turn_y(n, [(b, t) for t in range(PACK - 1) for b in range(BLOCKS)] + [(b, PACK - 1) for b in range(BLOCKS)])
+        round_y(n, 0, HALF, nc.vector.tensor_copy)
+        for b in range(BLOCKS):
+            copy_y(n, b)
+            if b == BLOCKS - 1:
+                quantise_y(n)
+                store_scales(y_scales_last, GROUPS - 1, GROUPS)
+            store_y(n, b, b + 1)

@@ -50,7 +50,7 @@ def tile_conformer_pointwise_glu_g4_kernel(
         warm_out = keep.tile([P, 8], F32, name="warm_out")
         x_first = [keep.tile([P, C], BF16, name="x_first%d" % b) for b in range(BLOCKS)]
         x_split = [keep.tile([P, C // 2], F32, name="x_split%d" % b) for b in range(BLOCKS)]
-        x_second = keep.tile([P, BLOCKS, C], BF16, name="x_second")
+        x_second = [keep.tile([P, 2, C], BF16, name="x_second%d" % j) for j in range(2)]
         x_grouped = [
             keep.tile([P, PASSES, HALF * PACK], BF16, name="x_grouped%d" % h, align_bytes=64) for h in range(HALVES)
         ]
@@ -58,13 +58,13 @@ def tile_conformer_pointwise_glu_g4_kernel(
         x_scales = [keep.tile([P, PASSES, HALF], U8, name="x_scales%d" % h, align_bytes=64) for h in range(HALVES)]
         raw_words = [keep.tile([P, 2, PASSES, 2 * SPAN], U8, name="raw_words%d" % g) for g in range(GROUPS)]
         raw_scales_first = keep.tile([P, 2, PASSES, SPAN], U8, name="raw_scales_first")
-        raw_scales_rest = keep.tile([P, 2, PASSES, D - SPAN], U8, name="raw_scales_rest")
+        rows_raw = keep.tile([P, D - SPAN], U8, name="rows_raw")
+        rows_ordered = keep.tile([P, D - SPAN], U8, name="rows_ordered")
         w_words = [
             keep.tile([P, PACK, 2, PASSES, 2 * P], U8, name="w_words%d" % g, align_bytes=64) for g in range(GROUPS)
         ]
-        w_scales = [
-            keep.tile([P, 2, PACK, PASSES, P], U8, name="w_scales%d" % g, align_bytes=64) for g in range(GROUPS)
-        ]
+        w_scales_first = keep.tile([P, 2, PASSES, SPAN], U8, name="w_scales_first", align_bytes=64)
+        w_scales_rest = keep.tile([P, 2, PASSES, D - SPAN], U8, name="w_scales_rest", align_bytes=64)
         bias = [keep.tile([P, GROUPS, PACK], BF16, name="bias%d" % w) for w in range(2)]
         y_scales_early = keep.tile([P, GROUPS - 1, TOKENS], U8, name="y_scales_early", align_bytes=64)
         y_scales_last = keep.tile([P, 1, TOKENS], U8, name="y_scales_last", align_bytes=64)
@@ -98,7 +98,7 @@ def tile_conformer_pointwise_glu_g4_kernel(
                     if h == 0:
                         src = x_split[b][:, (2 * k + u) * P : (2 * k + u + 1) * P]
                     else:
-                        src = x_second[:, b, :].bitcast(F32)[:, 2 * P * k + u : 2 * P * (k + 1) : 2]
+                        src = x_second[b // 2][:, b % 2, :].bitcast(F32)[:, 2 * P * k + u : 2 * P * (k + 1) : 2]
                     nc.tensor.transpose(bank[:, k, u, :], src, ident[:])
 
         def group_x(h, b):
@@ -120,12 +120,34 @@ def tile_conformer_pointwise_glu_g4_kernel(
                 in_=raw_words[g][:, ws].rearrange("p w k (m t e) -> p t (w k m) e", t=PACK, e=2)[:, t],
             )
 
-        def order_scales(g, w):
+        def order_first_scales(w):
+            nc.vector.tensor_copy(
+                out=w_scales_first[:, w].rearrange("p k (t m) -> p k t m", t=PACK),
+                in_=raw_scales_first[:, w].rearrange("p k (m t) -> p k t m", t=PACK),
+            )
+
+        def order_later_scales():
+            for g in range(GROUPS - 1):
+                nc.vector.tensor_copy(
+                    out=rows_ordered[:, SPAN * g : SPAN * (g + 1)].rearrange("p (t m) -> p t m", t=PACK),
+                    in_=rows_raw[:, SPAN * g : SPAN * (g + 1)].rearrange("p (m t) -> p t m", t=PACK),
+                )
+
+        def spread_later_scales():
+            for w in (GATE, VALUE):
+                for k in range(PASSES):
+                    for q in range(4):
+                        row = 64 * w + 16 * k + 4 * q
+                        nc.sync.dma_start(
+                            out=w_scales_rest[32 * q : 32 * q + 4, w, k, :].bitcast(I32),
+                            in_=rows_ordered[row : row + 4, :].bitcast(I32),
+                        )
+
+        def scale_plane(g, w, t, k):
             if g == 0:
-                src = raw_scales_first[:, w]
-            else:
-                src = raw_scales_rest[:, w, :, SPAN * (g - 1) : SPAN * g]
-            nc.vector.tensor_copy(out=w_scales[g][:, w], in_=src.rearrange("p k (m t) -> p t k m", t=PACK))
+                return w_scales_first[:, w, k, P * t : P * (t + 1)]
+            start = SPAN * (g - 1) + P * t
+            return w_scales_rest[:, w, k, start : start + P]
 
         def multiply(n, t):
             g, h = divmod(n, HALVES)
@@ -136,30 +158,33 @@ def tile_conformer_pointwise_glu_g4_kernel(
                     nc.tensor.matmul_mx(
                         out=acc[:],
                         lhsT=w_words[g][:, t, w, k, :].bitcast(FP4X4),
-                        lhsT_scale=w_scales[g][:, w, t, k, :],
+                        lhsT_scale=scale_plane(g, w, t, k),
                         rhs=x_codes[h][:, k, :].bitcast(FP8X4),
                         rhs_scale=x_scales[h][:, k, :],
                         start=(k == 0),
                         stop=(k == PASSES - 1),
                     )
 
-        def sigmoid(n, t):
+        def sigmoid(n, t, lo=0, hi=HALF):
             g = n // HALVES
-            sig = work.tile([P, HALF], F32, name="sig", tag="sig", bufs=3)
-            live["sig", n, t] = sig
+            if lo == 0:
+                live["sig", n, t] = work.tile([P, HALF], F32, name="sig", tag="sig", bufs=3)
             nc.scalar.activation(
-                out=sig[:], in_=live["acc", GATE, n, t][:], func=ACT.Sigmoid, bias=bias[GATE][:, g, t : t + 1]
+                out=live["sig", n, t][:, lo:hi],
+                in_=live["acc", GATE, n, t][:, lo:hi],
+                func=ACT.Sigmoid,
+                bias=bias[GATE][:, g, t : t + 1],
             )
 
-        def product(n, t):
+        def product(n, t, lo=0, hi=HALF):
             g = n // HALVES
             if t == 0:
                 live["yt", n] = work.tile([P, PACK, HALF], F32, name="yt", tag="yt", bufs=2)
             nc.vector.scalar_tensor_tensor(
-                out=live["yt", n][:, t, :],
-                in0=live["acc", VALUE, n, t][:],
+                out=live["yt", n][:, t, lo:hi],
+                in0=live["acc", VALUE, n, t][:, lo:hi],
                 scalar=bias[VALUE][:, g, t : t + 1],
-                in1=live["sig", n, t][:],
+                in1=live["sig", n, t][:, lo:hi],
                 op0=ALU.add,
                 op1=ALU.mult,
             )
@@ -193,20 +218,26 @@ def tile_conformer_pointwise_glu_g4_kernel(
             if ("yb", n) not in live:
                 live["yb", n] = work.tile([P, HALF * PACK], BF16, name="yb", tag="yb", bufs=2, align_bytes=64)
             copy(
-                out=live["yb", n][:, PACK * lo : PACK * hi].rearrange("p (c i t) -> p c t i", i=4, t=PACK),
-                in_=live["yt", n][:, :, lo:hi].rearrange("p t (c i) -> p c t i", i=4),
+                out=live["yb", n][:, PACK * lo : PACK * hi].rearrange("p (c i t) -> p c t i", i=2, t=PACK),
+                in_=live["yt", n][:, :, lo:hi].rearrange("p t (c i) -> p c t i", i=2),
             )
 
-        def quantise_y(n):
+        def quantise_y(n, lo=0, hi=HALF):
             g, h = divmod(n, HALVES)
-            codes = work.tile([P, HALF], U32, name="y_codes", tag="y_codes", bufs=3, align_bytes=64)
+            if lo == 0:
+                live["codes", n] = work.tile([P, HALF], U32, name="y_codes", tag="y_codes", bufs=3, align_bytes=64)
             plane = y_scales_early[:, g] if g < GROUPS - 1 else y_scales_last[:, 0]
             nc.vector.quantize_mx(
-                out=codes[:].bitcast(FP8X4), scales=plane[:, HALF * h : HALF * (h + 1)], in_=live["yb", n][:]
+                out=live["codes", n][:, lo:hi].bitcast(FP8X4),
+                scales=plane[:, HALF * h + lo : HALF * h + hi],
+                in_=live["yb", n][:, PACK * lo : PACK * hi],
             )
+
+        def store_codes(n):
+            g, h = divmod(n, HALVES)
             nc.sync.dma_start(
                 out=out_1[g, :, HALF * h : HALF * (h + 1), :].rearrange("p m t -> p (m t)").bitcast(I32),
-                in_=codes[:].bitcast(I32),
+                in_=live["codes", n][:].bitcast(I32),
             )
 
         def store_scales(tile, lo, hi):
@@ -223,7 +254,8 @@ def tile_conformer_pointwise_glu_g4_kernel(
         make_identity(nc, ident[:])
         load_scales(nc.scalar, raw_scales_first, GATE, slice(0, SPAN))
         nc.scalar.activation(out=warm_out[:], in_=warm_in[:], func=ACT.Sigmoid)
-        nc.vector.memset(raw_scales_rest[:].rearrange("p w k n -> p (w k n)").bitcast(I32), 0)
+        nc.vector.memset(rows_raw[:].bitcast(I32), 0)
+        nc.vector.memset(w_scales_rest[:].rearrange("p w k n -> p (w k n)").bitcast(I32), 0)
         for b in range(BLOCKS):
             nc.sync.dma_start(out=x_first[b][:], in_=x_rows[P * b : P * (b + 1), :])
         load_words(0, GATE)
@@ -231,9 +263,14 @@ def tile_conformer_pointwise_glu_g4_kernel(
         load_scales(nc.sync, raw_scales_first, VALUE, slice(0, SPAN))
         for w in (GATE, VALUE):
             nc.sync.dma_start(out=bias[w][:], in_=bias_in[w].rearrange("(g p t) -> p g t", p=P, t=PACK))
-        nc.sync.dma_start(out=x_second[:], in_=x_rows[HALF:, :].rearrange("(b r) c -> r b c", r=P))
+        for j in range(2):
+            rows = x_rows[HALF + 2 * P * j : HALF + 2 * P * (j + 1), :]
+            nc.sync.dma_start(out=x_second[j][:], in_=rows.rearrange("(b r) c -> r b c", r=P))
         for w in (GATE, VALUE):
-            load_scales(nc.sync, raw_scales_rest, w, slice(SPAN, D))
+            nc.sync.dma_start(
+                out=rows_raw[64 * w : 64 * w + 32, :].bitcast(I32),
+                in_=scales_in[w].rearrange("k q n -> (k q) n")[:, SPAN:].bitcast(I32),
+            )
         for g in range(1, GROUPS):
             load_words(g, GATE)
             load_words(g, VALUE)
@@ -241,79 +278,89 @@ def tile_conformer_pointwise_glu_g4_kernel(
         for b in range(BLOCKS):
             split_x(b)
             if b == 1:
-                order_scales(0, GATE)
+                order_first_scales(GATE)
             turn_x(0, b)
             group_x(0, b)
+        order_words(0, 0, slice(GATE, GATE + 1))
         for b in range(BLOCKS - 1):
             for k in range(PASSES):
                 quantise_x(0, k, P * b, P * (b + 1))
-        order_words(0, 0, slice(GATE, GATE + 1))
+            if b == 0:
+                order_first_scales(VALUE)
+            if b == 1:
+                order_words(0, 0, slice(VALUE, VALUE + 1))
         for k in range(PASSES):
             quantise_x(0, k, P * (BLOCKS - 1), HALF)
-        order_words(0, 0, slice(VALUE, VALUE + 1))
-        order_scales(0, VALUE)
 
         step(0, 0)
         order_words(0, 1, both)
-        step(0, 1)
-        product(0, 0)
         order_words(0, 2, both)
         for b in range(BLOCKS):
             turn_x(1, b)
-        group_x(1, 0)
-        group_x(1, 1)
-        product(0, 1)
+            group_x(1, b)
+        product(0, 0)
         order_words(0, 3, both)
+        order_later_scales()
+        spread_later_scales()
+        step(0, 1)
+        quantise_x(1, 0, 0, HALF)
+        product(0, 1)
+        quantise_x(1, 1, 0, HALF)
         step(0, 2)
-        group_x(1, 2)
-        group_x(1, 3)
-        step(0, 3)
         product(0, 2)
-        for k in range(PASSES):
-            quantise_x(1, k, 0, HALF)
+        step(0, 3)
 
         block_major = [(b, t) for b in range(BLOCKS) for t in range(PACK)]
         for n in range(1, UNITS):
             g, h = divmod(n, HALVES)
             if h == 0:
-                chores = [lambda t=t, g=g: order_words(g, t, both) for t in (1, 2, 3)]
+                chores = [lambda g=g: order_words(g, 2, both), lambda g=g: order_words(g, 3, both)]
             elif g + 1 < GROUPS:
-                chores = [
-                    lambda g=g: order_scales(g + 1, GATE),
-                    lambda g=g: order_scales(g + 1, VALUE),
-                    lambda g=g: order_words(g + 1, 0, both),
-                ]
+                chores = [lambda g=g: order_words(g + 1, 0, both), lambda g=g: order_words(g + 1, 1, both)]
             else:
-                chores = [lambda: None] * 3
+                chores = [lambda: None] * 2
             product(n - 1, 3)
             step(n, 0)
             chores[0]()
-            round_y(n - 1, CAST_SPLIT, HALF, nc.scalar.copy)
+            split = CAST_SPLIT if n < UNITS - 1 else HALF
+            if split < HALF:
+                round_y(n - 1, split, HALF, nc.scalar.copy)
             turn_y(n - 1, block_major)
             product(n, 0)
+            round_y(n - 1, 0, split, nc.vector.tensor_copy)
             chores[1]()
-            round_y(n - 1, 0, CAST_SPLIT, nc.vector.tensor_copy)
-            chores[2]()
-            for b in range(3):
-                copy_y(n - 1, b)
+            copy_y(n - 1, 0)
+            copy_y(n - 1, 1)
+            store_y(n - 1, 0, 2)
             step(n, 1)
-            copy_y(n - 1, 3)
-            store_y(n - 1, 0, BLOCKS)
+            copy_y(n - 1, 2)
             product(n, 1)
             quantise_y(n - 1)
+            store_codes(n - 1)
             if n == UNITS - 2:
                 store_scales(y_scales_early, 0, GROUPS - 1)
             step(n, 2)
+            copy_y(n - 1, 3)
+            store_y(n - 1, 2, BLOCKS)
             product(n, 2)
-            step(n, 3)
+            if n < UNITS - 1:
+                step(n, 3)
 
         n = UNITS - 1
-        product(n, 3)
-        turn_y(n, [(b, t) for t in range(PACK - 1) for b in range(BLOCKS)] + [(b, PACK - 1) for b in range(BLOCKS)])
-        round_y(n, 0, HALF, nc.vector.tensor_copy)
+        mid = HALF // 2
+        multiply(n, 3)
+        sigmoid(n, 3, 0, mid)
+        sigmoid(n, 3, mid, HALF)
+        product(n, 3, 0, mid)
+        product(n, 3, mid, HALF)
+        turn_y(n, [(b, t) for b in (0, 1) for t in range(3)] + [(2, 0), (2, 1), (0, 3), (1, 3), (2, 2), (3, 0), (3, 1), (3, 2), (2, 3), (3, 3)])
+        round_y(n, 0, mid, nc.vector.tensor_copy)
+        round_y(n, mid, HALF, nc.vector.tensor_copy)
+        quantise_y(n, 0, mid)
+        quantise_y(n, mid, HALF)
         for b in range(BLOCKS):
             copy_y(n, b)
             if b == BLOCKS - 1:
-                quantise_y(n)
-                store_scales(y_scales_last, GROUPS - 1, GROUPS)
+                store_codes(n)
             store_y(n, b, b + 1)
+        store_scales(y_scales_last, GROUPS - 1, GROUPS)

@@ -26,7 +26,6 @@ HALVES = TOKENS // HALF
 BLOCKS = HALF // P
 UNITS = GROUPS * HALVES
 GATE, VALUE = 0, 1
-CAST_SPLIT = 384
 
 
 def tile_conformer_pointwise_glu_g4_kernel(
@@ -49,7 +48,7 @@ def tile_conformer_pointwise_glu_g4_kernel(
         warm_in = keep.tile([P, 8], F32, name="warm_in")
         warm_out = keep.tile([P, 8], F32, name="warm_out")
         x_first = [keep.tile([P, C], BF16, name="x_first%d" % b) for b in range(BLOCKS)]
-        x_split = [keep.tile([P, C // 2], F32, name="x_split%d" % b) for b in range(BLOCKS)]
+        x_split = [keep.tile([P, C // 2], F32, name="x_split%d" % b) for b in range(HALVES * BLOCKS)]
         x_second = [keep.tile([P, 2, C], BF16, name="x_second%d" % j) for j in range(2)]
         x_grouped = [
             keep.tile([P, PASSES, HALF * PACK], BF16, name="x_grouped%d" % h, align_bytes=64) for h in range(HALVES)
@@ -84,10 +83,11 @@ def tile_conformer_pointwise_glu_g4_kernel(
                 in_=words_in[w][:, :, 2 * SPAN * g : 2 * SPAN * (g + 1)].rearrange("k p n -> p k n").bitcast(I32),
             )
 
-        def split_x(b):
+        def split_x(h, b):
+            rows = x_first[b][:] if h == 0 else x_second[b // 2][:, b % 2, :]
             nc.vector.tensor_copy(
-                out=x_split[b][:].rearrange("r (k u p) -> r k u p", k=PASSES, u=2),
-                in_=x_first[b][:].bitcast(F32).rearrange("r (k p u) -> r k u p", k=PASSES, u=2),
+                out=x_split[BLOCKS * h + b][:].rearrange("r (k u p) -> r k u p", k=PASSES, u=2),
+                in_=rows.bitcast(F32).rearrange("r (k p u) -> r k u p", k=PASSES, u=2),
             )
 
         def turn_x(h, b):
@@ -95,10 +95,7 @@ def tile_conformer_pointwise_glu_g4_kernel(
             live["x", h, b] = bank
             for k in range(PASSES):
                 for u in range(2):
-                    if h == 0:
-                        src = x_split[b][:, (2 * k + u) * P : (2 * k + u + 1) * P]
-                    else:
-                        src = x_second[b // 2][:, b % 2, :].bitcast(F32)[:, 2 * P * k + u : 2 * P * (k + 1) : 2]
+                    src = x_split[BLOCKS * h + b][:, (2 * k + u) * P : (2 * k + u + 1) * P]
                     nc.tensor.transpose(bank[:, k, u, :], src, ident[:])
 
         def group_x(h, b):
@@ -205,8 +202,8 @@ def tile_conformer_pointwise_glu_g4_kernel(
             if b == 0:
                 live["y", n] = work.tile([P, BLOCKS, SPAN], F32, name="y", tag="y", bufs=3)
             nc.scalar.copy(
-                out=live["y", n][:, b, :].rearrange("r (p t) -> r p t", t=PACK),
-                in_=live["turn", n, b][:].rearrange("r t p -> r p t"),
+                out=live["y", n][:, b, :].rearrange("r (c i t) -> r c t i", i=2, t=PACK),
+                in_=live["turn", n, b][:].rearrange("r t (c i) -> r c t i", i=2),
             )
 
         def store_y(n, lo, hi):
@@ -276,7 +273,7 @@ def tile_conformer_pointwise_glu_g4_kernel(
             load_words(g, VALUE)
 
         for b in range(BLOCKS):
-            split_x(b)
+            split_x(0, b)
             if b == 1:
                 order_first_scales(GATE)
             turn_x(0, b)
@@ -294,20 +291,23 @@ def tile_conformer_pointwise_glu_g4_kernel(
 
         step(0, 0)
         order_words(0, 1, both)
-        order_words(0, 2, both)
         for b in range(BLOCKS):
+            split_x(1, b)
             turn_x(1, b)
+        for b in range(BLOCKS - 1):
             group_x(1, b)
         product(0, 0)
+        order_words(0, 2, both)
         order_words(0, 3, both)
         order_later_scales()
         spread_later_scales()
         step(0, 1)
-        quantise_x(1, 0, 0, HALF)
+        group_x(1, BLOCKS - 1)
         product(0, 1)
-        quantise_x(1, 1, 0, HALF)
+        quantise_x(1, 0, 0, HALF)
         step(0, 2)
         product(0, 2)
+        quantise_x(1, 1, 0, HALF)
         step(0, 3)
 
         block_major = [(b, t) for b in range(BLOCKS) for t in range(PACK)]
@@ -322,12 +322,9 @@ def tile_conformer_pointwise_glu_g4_kernel(
             product(n - 1, 3)
             step(n, 0)
             chores[0]()
-            split = CAST_SPLIT if n < UNITS - 1 else HALF
-            if split < HALF:
-                round_y(n - 1, split, HALF, nc.scalar.copy)
             turn_y(n - 1, block_major)
             product(n, 0)
-            round_y(n - 1, 0, split, nc.vector.tensor_copy)
+            round_y(n - 1, 0, HALF, nc.vector.tensor_copy)
             chores[1]()
             copy_y(n - 1, 0)
             copy_y(n - 1, 1)

@@ -26,6 +26,7 @@ HALVES = TOKENS // HALF
 BLOCKS = HALF // P
 UNITS = GROUPS * HALVES
 GATE, VALUE = 0, 1
+FIRST_ORDER = [(GATE, 0), (GATE, 1), (GATE, 2), (VALUE, 0), (VALUE, 1), (GATE, 3), (VALUE, 2), (VALUE, 3)]
 
 
 def tile_conformer_pointwise_glu_g4_kernel(
@@ -83,9 +84,9 @@ def tile_conformer_pointwise_glu_g4_kernel(
                 in_=words_in[w][:, :, 2 * SPAN * g : 2 * SPAN * (g + 1)].rearrange("k p n -> p k n").bitcast(I32),
             )
 
-        def split_x(h, b):
+        def split_x(h, b, copy):
             rows = x_first[b][:] if h == 0 else x_second[b // 2][:, b % 2, :]
-            nc.vector.tensor_copy(
+            copy(
                 out=x_split[BLOCKS * h + b][:].rearrange("r (k u p) -> r k u p", k=PASSES, u=2),
                 in_=rows.bitcast(F32).rearrange("r (k p u) -> r k u p", k=PASSES, u=2),
             )
@@ -146,21 +147,24 @@ def tile_conformer_pointwise_glu_g4_kernel(
             start = SPAN * (g - 1) + P * t
             return w_scales_rest[:, w, k, start : start + P]
 
-        def multiply(n, t):
+        def accumulate(n, t, w, lo, hi):
             g, h = divmod(n, HALVES)
+            if lo == 0:
+                live["acc", w, n, t] = psum.tile([P, HALF], F32, name="acc%d" % w, tag="acc%d" % w, bufs=2)
+            for k in range(PASSES):
+                nc.tensor.matmul_mx(
+                    out=live["acc", w, n, t][:, lo:hi],
+                    lhsT=w_words[g][:, t, w, k, :].bitcast(FP4X4),
+                    lhsT_scale=scale_plane(g, w, t, k),
+                    rhs=x_codes[h][:, k, lo:hi].bitcast(FP8X4),
+                    rhs_scale=x_scales[h][:, k, lo:hi],
+                    start=(k == 0),
+                    stop=(k == PASSES - 1),
+                )
+
+        def multiply(n, t):
             for w in (GATE, VALUE):
-                acc = psum.tile([P, HALF], F32, name="acc%d" % w, tag="acc%d" % w, bufs=2)
-                live["acc", w, n, t] = acc
-                for k in range(PASSES):
-                    nc.tensor.matmul_mx(
-                        out=acc[:],
-                        lhsT=w_words[g][:, t, w, k, :].bitcast(FP4X4),
-                        lhsT_scale=scale_plane(g, w, t, k),
-                        rhs=x_codes[h][:, k, :].bitcast(FP8X4),
-                        rhs_scale=x_scales[h][:, k, :],
-                        start=(k == 0),
-                        stop=(k == PASSES - 1),
-                    )
+                accumulate(n, t, w, 0, HALF)
 
         def sigmoid(n, t, lo=0, hi=HALF):
             g = n // HALVES
@@ -198,10 +202,10 @@ def tile_conformer_pointwise_glu_g4_kernel(
                     live["turn", n, b][:, t, :], live["yt", n][:, t, P * b : P * (b + 1)], ident[:]
                 )
 
-        def copy_y(n, b):
+        def copy_y(n, b, copy=nc.scalar.copy):
             if b == 0:
                 live["y", n] = work.tile([P, BLOCKS, SPAN], F32, name="y", tag="y", bufs=3)
-            nc.scalar.copy(
+            copy(
                 out=live["y", n][:, b, :].rearrange("r (c i t) -> r c t i", i=2, t=PACK),
                 in_=live["turn", n, b][:].rearrange("r t (c i) -> r c t i", i=2),
             )
@@ -273,42 +277,44 @@ def tile_conformer_pointwise_glu_g4_kernel(
             load_words(g, VALUE)
 
         for b in range(BLOCKS):
-            split_x(0, b)
+            split_x(0, b, nc.vector.tensor_copy)
             if b == 1:
                 order_first_scales(GATE)
             turn_x(0, b)
             group_x(0, b)
-        order_words(0, 0, slice(GATE, GATE + 1))
-        for b in range(BLOCKS - 1):
+        for b in range(BLOCKS):
             for k in range(PASSES):
                 quantise_x(0, k, P * b, P * (b + 1))
             if b == 0:
-                order_first_scales(VALUE)
+                order_words(0, 0, slice(GATE, GATE + 1))
             if b == 1:
+                order_first_scales(VALUE)
+            if b == 2:
                 order_words(0, 0, slice(VALUE, VALUE + 1))
-        for k in range(PASSES):
-            quantise_x(0, k, P * (BLOCKS - 1), HALF)
 
-        step(0, 0)
+        for w, b in FIRST_ORDER:
+            accumulate(0, 0, w, P * b, P * (b + 1))
+        sigmoid(0, 0)
+        split_x(1, 3, nc.scalar.copy)
         order_words(0, 1, both)
-        for b in range(BLOCKS):
-            split_x(1, b)
-            turn_x(1, b)
-        for b in range(BLOCKS - 1):
-            group_x(1, b)
+        step(0, 1)
+        split_x(1, 0, nc.vector.tensor_copy)
+        split_x(1, 1, nc.vector.tensor_copy)
+        split_x(1, 2, nc.vector.tensor_copy)
         product(0, 0)
         order_words(0, 2, both)
+        for b in range(BLOCKS):
+            turn_x(1, b)
+            group_x(1, b)
+        product(0, 1)
         order_words(0, 3, both)
         order_later_scales()
         spread_later_scales()
-        step(0, 1)
-        group_x(1, BLOCKS - 1)
-        product(0, 1)
-        quantise_x(1, 0, 0, HALF)
         step(0, 2)
-        product(0, 2)
+        quantise_x(1, 0, 0, HALF)
         quantise_x(1, 1, 0, HALF)
         step(0, 3)
+        product(0, 2)
 
         block_major = [(b, t) for b in range(BLOCKS) for t in range(PACK)]
         for n in range(1, UNITS):
@@ -353,8 +359,7 @@ def tile_conformer_pointwise_glu_g4_kernel(
         turn_y(n, [(b, t) for b in (0, 1) for t in range(3)] + [(2, 0), (2, 1), (0, 3), (1, 3), (2, 2), (3, 0), (3, 1), (3, 2), (2, 3), (3, 3)])
         round_y(n, 0, mid, nc.vector.tensor_copy)
         round_y(n, mid, HALF, nc.vector.tensor_copy)
-        quantise_y(n, 0, mid)
-        quantise_y(n, mid, HALF)
+        quantise_y(n, 0, HALF)
         for b in range(BLOCKS):
             copy_y(n, b)
             if b == BLOCKS - 1:

from contextlib import ExitStack

import concourse.mybir as mybir
from concourse.masks import make_identity

F32 = mybir.dt.float32
BF16 = mybir.dt.bfloat16
I32 = mybir.dt.int32
U32 = mybir.dt.uint32
U8 = mybir.dt.uint8
FP8X4 = mybir.dt.float8_e4m3fn_x4
FP4X4 = mybir.dt.float4_e2m1fn_x4
ACT = mybir.ActivationFunctionType
ALU = mybir.AluOpType

TOKENS, C, D = 1024, 1024, 2048
FLOPS = 2 * 2 * TOKENS * C * D

P = 128
PACK = 4
SPAN = P * PACK
PASSES = C // SPAN
GROUPS = D // SPAN
HALF = 512
HALVES = TOKENS // HALF
BLOCKS = HALF // P
UNITS = GROUPS * HALVES
GATE, VALUE = 0, 1
FIRST_ORDER = [(GATE, 0), (GATE, 1), (GATE, 2), (VALUE, 0), (VALUE, 1), (GATE, 3), (VALUE, 2), (VALUE, 3)]


def tile_conformer_pointwise_glu_g4_kernel(
    tc, x, wv_words, wv_scales, wg_words, wg_scales, value_bias, gate_bias, out_0, out_1, out_2
):
    nc = tc.nc
    x_rows = x.rearrange("b f c -> (b f) c")
    y_rows = out_0.rearrange("b f d -> (b f) d")
    words_in = {GATE: wg_words, VALUE: wv_words}
    scales_in = {GATE: wg_scales, VALUE: wv_scales}
    bias_in = {GATE: gate_bias, VALUE: value_bias}

    with ExitStack() as ctx:
        keep = ctx.enter_context(tc.tile_pool(name="keep", bufs=1))
        work = ctx.enter_context(tc.tile_pool(name="work", bufs=2))
        psum = ctx.enter_context(tc.psum_pool(name="psum", bufs=2))
        ctx.enter_context(tc.manual_schedule())

        ident = keep.tile([P, P], F32, name="ident")
        warm_in = keep.tile([P, 8], F32, name="warm_in")
        warm_out = keep.tile([P, 8], F32, name="warm_out")
        x_first = [keep.tile([P, C], BF16, name="x_first%d" % b) for b in range(BLOCKS)]
        x_split = [keep.tile([P, C // 2], F32, name="x_split%d" % b) for b in range(HALVES * BLOCKS)]
        x_second = [keep.tile([P, 2, C], BF16, name="x_second%d" % j) for j in range(2)]
        x_grouped = [
            keep.tile([P, PASSES, HALF * PACK], BF16, name="x_grouped%d" % h, align_bytes=64) for h in range(HALVES)
        ]
        x_codes = [keep.tile([P, PASSES, HALF], U32, name="x_codes%d" % h, align_bytes=64) for h in range(HALVES)]
        x_scales = [keep.tile([P, PASSES, HALF], U8, name="x_scales%d" % h, align_bytes=64) for h in range(HALVES)]
        raw_words = [keep.tile([P, 2, PASSES, 2 * SPAN], U8, name="raw_words%d" % g) for g in range(GROUPS)]
        raw_scales_first = keep.tile([P, 2, PASSES, SPAN], U8, name="raw_scales_first")
        rows_raw = keep.tile([P, D - SPAN], U8, name="rows_raw")
        rows_ordered = keep.tile([P, D - SPAN], U8, name="rows_ordered")
        w_words = [
            keep.tile([P, PACK, 2, PASSES, 2 * P], U8, name="w_words%d" % g, align_bytes=64) for g in range(GROUPS)
        ]
        w_scales_first = keep.tile([P, 2, PASSES, SPAN], U8, name="w_scales_first", align_bytes=64)
        w_scales_rest = keep.tile([P, 2, PASSES, D - SPAN], U8, name="w_scales_rest", align_bytes=64)
        bias = [keep.tile([P, GROUPS, PACK], BF16, name="bias%d" % w) for w in range(2)]
        y_scales_early = keep.tile([P, GROUPS - 1, TOKENS], U8, name="y_scales_early", align_bytes=64)
        y_scales_last = keep.tile([P, 1, TOKENS], U8, name="y_scales_last", align_bytes=64)

        live = {}

        def load_scales(queue, tile, w, cols):
            for q in range(4):
                queue.dma_start(
                    out=tile[32 * q : 32 * q + 4, w].bitcast(I32),
                    in_=scales_in[w][:, 4 * q : 4 * q + 4, cols].rearrange("k r n -> r k n").bitcast(I32),
                )

        def load_words(g, w):
            nc.sync.dma_start(
                out=raw_words[g][:, w].bitcast(I32),
                in_=words_in[w][:, :, 2 * SPAN * g : 2 * SPAN * (g + 1)].rearrange("k p n -> p k n").bitcast(I32),
            )

        def split_x(h, b, copy):
            rows = x_first[b][:] if h == 0 else x_second[b // 2][:, b % 2, :]
            copy(
                out=x_split[BLOCKS * h + b][:].rearrange("r (k u p) -> r k u p", k=PASSES, u=2),
                in_=rows.bitcast(F32).rearrange("r (k p u) -> r k u p", k=PASSES, u=2),
            )

        def turn_x(h, b):
            bank = psum.tile([P, PASSES, 2, P], F32, name="turn", tag="turn", bufs=4)
            live["x", h, b] = bank
            for k in range(PASSES):
                for u in range(2):
                    src = x_split[BLOCKS * h + b][:, (2 * k + u) * P : (2 * k + u + 1) * P]
                    nc.tensor.transpose(bank[:, k, u, :], src, ident[:])

        def group_x(h, b):
            nc.scalar.copy(
                out=x_grouped[h][:, :, SPAN * b : SPAN * (b + 1)].bitcast(F32).rearrange("p k (r u) -> p k r u", u=2),
                in_=live["x", h, b][:].rearrange("p k u r -> p k r u"),
            )

        def quantise_x(h, k, lo, hi):
            nc.vector.quantize_mx(
                out=x_codes[h][:, k, lo:hi].bitcast(FP8X4),
                scales=x_scales[h][:, k, lo:hi],
                in_=x_grouped[h][:, k, PACK * lo : PACK * hi],
            )

        def order_words(g, t, ws):
            nc.vector.tensor_copy(
                out=w_words[g][:, t, ws].rearrange("p w k (m e) -> p (w k m) e", e=2),
                in_=raw_words[g][:, ws].rearrange("p w k (m t e) -> p t (w k m) e", t=PACK, e=2)[:, t],
            )

        def order_first_scales(w):
            nc.vector.tensor_copy(
                out=w_scales_first[:, w].rearrange("p k (t m) -> p k t m", t=PACK),
                in_=raw_scales_first[:, w].rearrange("p k (m t) -> p k t m", t=PACK),
            )

        def order_later_scales():
            for g in range(GROUPS - 1):
                nc.vector.tensor_copy(
                    out=rows_ordered[:, SPAN * g : SPAN * (g + 1)].rearrange("p (t m) -> p t m", t=PACK),
                    in_=rows_raw[:, SPAN * g : SPAN * (g + 1)].rearrange("p (m t) -> p t m", t=PACK),
                )

        def spread_later_scales():
            for w in (GATE, VALUE):
                for k in range(PASSES):
                    for q in range(4):
                        row = 64 * w + 16 * k + 4 * q
                        nc.sync.dma_start(
                            out=w_scales_rest[32 * q : 32 * q + 4, w, k, :].bitcast(I32),
                            in_=rows_ordered[row : row + 4, :].bitcast(I32),
                        )

        def scale_plane(g, w, t, k):
            if g == 0:
                return w_scales_first[:, w, k, P * t : P * (t + 1)]
            start = SPAN * (g - 1) + P * t
            return w_scales_rest[:, w, k, start : start + P]

        def accumulate(n, t, w, lo, hi):
            g, h = divmod(n, HALVES)
            if lo == 0:
                live["acc", w, n, t] = psum.tile([P, HALF], F32, name="acc%d" % w, tag="acc%d" % w, bufs=2)
            for k in range(PASSES):
                nc.tensor.matmul_mx(
                    out=live["acc", w, n, t][:, lo:hi],
                    lhsT=w_words[g][:, t, w, k, :].bitcast(FP4X4),
                    lhsT_scale=scale_plane(g, w, t, k),
                    rhs=x_codes[h][:, k, lo:hi].bitcast(FP8X4),
                    rhs_scale=x_scales[h][:, k, lo:hi],
                    start=(k == 0),
                    stop=(k == PASSES - 1),
                )

        def multiply(n, t):
            for w in (GATE, VALUE):
                accumulate(n, t, w, 0, HALF)

        def sigmoid(n, t, lo=0, hi=HALF):
            g = n // HALVES
            if lo == 0:
                live["sig", n, t] = work.tile([P, HALF], F32, name="sig", tag="sig", bufs=3)
            nc.scalar.activation(
                out=live["sig", n, t][:, lo:hi],
                in_=live["acc", GATE, n, t][:, lo:hi],
                func=ACT.Sigmoid,
                bias=bias[GATE][:, g, t : t + 1],
            )

        def product(n, t, lo=0, hi=HALF):
            g = n // HALVES
            if t == 0:
                live["yt", n] = work.tile([P, PACK, HALF], F32, name="yt", tag="yt", bufs=2)
            nc.vector.scalar_tensor_tensor(
                out=live["yt", n][:, t, lo:hi],
                in0=live["acc", VALUE, n, t][:, lo:hi],
                scalar=bias[VALUE][:, g, t : t + 1],
                in1=live["sig", n, t][:, lo:hi],
                op0=ALU.add,
                op1=ALU.mult,
            )

        def step(n, t):
            multiply(n, t)
            sigmoid(n, t)

        def turn_y(n, order):
            for b in range(BLOCKS):
                live["turn", n, b] = psum.tile([P, PACK, P], F32, name="turn", tag="turn", bufs=4)
            for b, t in order:
                nc.tensor.transpose(
                    live["turn", n, b][:, t, :], live["yt", n][:, t, P * b : P * (b + 1)], ident[:]
                )

        def copy_y(n, b, copy=nc.scalar.copy):
            if b == 0:
                live["y", n] = work.tile([P, BLOCKS, SPAN], F32, name="y", tag="y", bufs=3)
            copy(
                out=live["y", n][:, b, :].rearrange("r (c i t) -> r c t i", i=2, t=PACK),
                in_=live["turn", n, b][:].rearrange("r t (c i) -> r c t i", i=2),
            )

        def store_y(n, lo, hi):
            g, h = divmod(n, HALVES)
            rows = y_rows[HALF * h + P * lo : HALF * h + P * hi, SPAN * g : SPAN * (g + 1)]
            nc.sync.dma_start(out=rows.rearrange("(b r) d -> r b d", r=P), in_=live["y", n][:, lo:hi, :])

        def round_y(n, lo, hi, copy):
            if ("yb", n) not in live:
                live["yb", n] = work.tile([P, HALF * PACK], BF16, name="yb", tag="yb", bufs=2, align_bytes=64)
            copy(
                out=live["yb", n][:, PACK * lo : PACK * hi].rearrange("p (c i t) -> p c t i", i=2, t=PACK),
                in_=live["yt", n][:, :, lo:hi].rearrange("p t (c i) -> p c t i", i=2),
            )

        def quantise_y(n, lo=0, hi=HALF):
            g, h = divmod(n, HALVES)
            if lo == 0:
                live["codes", n] = work.tile([P, HALF], U32, name="y_codes", tag="y_codes", bufs=3, align_bytes=64)
            plane = y_scales_early[:, g] if g < GROUPS - 1 else y_scales_last[:, 0]
            nc.vector.quantize_mx(
                out=live["codes", n][:, lo:hi].bitcast(FP8X4),
                scales=plane[:, HALF * h + lo : HALF * h + hi],
                in_=live["yb", n][:, PACK * lo : PACK * hi],
            )

        def store_codes(n):
            g, h = divmod(n, HALVES)
            nc.sync.dma_start(
                out=out_1[g, :, HALF * h : HALF * (h + 1), :].rearrange("p m t -> p (m t)").bitcast(I32),
                in_=live["codes", n][:].bitcast(I32),
            )

        def store_scales(tile, lo, hi):
            for q in range(4):
                nc.sync.dma_start(
                    out=out_2[lo:hi, 4 * q : 4 * q + 4, :].rearrange("g r m -> r g m").bitcast(I32),
                    in_=tile[32 * q : 32 * q + 4].bitcast(I32),
                )

        both = slice(0, 2)

        nc.vector.memset(raw_scales_first[:].rearrange("p w k n -> p (w k n)").bitcast(I32), 0)
        nc.vector.memset(warm_in[:], 0.0)
        make_identity(nc, ident[:])
        load_scales(nc.scalar, raw_scales_first, GATE, slice(0, SPAN))
        nc.scalar.activation(out=warm_out[:], in_=warm_in[:], func=ACT.Sigmoid)
        nc.vector.memset(rows_raw[:].bitcast(I32), 0)
        nc.vector.memset(w_scales_rest[:].rearrange("p w k n -> p (w k n)").bitcast(I32), 0)
        for b in range(BLOCKS):
            nc.sync.dma_start(out=x_first[b][:], in_=x_rows[P * b : P * (b + 1), :])
        load_words(0, GATE)
        load_words(0, VALUE)
        load_scales(nc.sync, raw_scales_first, VALUE, slice(0, SPAN))
        for w in (GATE, VALUE):
            nc.sync.dma_start(out=bias[w][:], in_=bias_in[w].rearrange("(g p t) -> p g t", p=P, t=PACK))
        for j in range(2):
            rows = x_rows[HALF + 2 * P * j : HALF + 2 * P * (j + 1), :]
            nc.sync.dma_start(out=x_second[j][:], in_=rows.rearrange("(b r) c -> r b c", r=P))
        for w in (GATE, VALUE):
            nc.sync.dma_start(
                out=rows_raw[64 * w : 64 * w + 32, :].bitcast(I32),
                in_=scales_in[w].rearrange("k q n -> (k q) n")[:, SPAN:].bitcast(I32),
            )
        for g in range(1, GROUPS):
            load_words(g, GATE)
            load_words(g, VALUE)

        for b in range(BLOCKS):
            split_x(0, b, nc.vector.tensor_copy)
            if b == 1:
                order_first_scales(GATE)
            turn_x(0, b)
            group_x(0, b)
        for b in range(BLOCKS):
            for k in range(PASSES):
                quantise_x(0, k, P * b, P * (b + 1))
            if b == 0:
                order_words(0, 0, slice(GATE, GATE + 1))
            if b == 1:
                order_first_scales(VALUE)
            if b == 2:
                order_words(0, 0, slice(VALUE, VALUE + 1))

        for w, b in FIRST_ORDER:
            accumulate(0, 0, w, P * b, P * (b + 1))
        sigmoid(0, 0)
        split_x(1, 3, nc.scalar.copy)
        order_words(0, 1, both)
        step(0, 1)
        split_x(1, 0, nc.vector.tensor_copy)
        split_x(1, 1, nc.vector.tensor_copy)
        split_x(1, 2, nc.vector.tensor_copy)
        product(0, 0)
        order_words(0, 2, both)
        for b in range(BLOCKS):
            turn_x(1, b)
            group_x(1, b)
        product(0, 1)
        order_words(0, 3, both)
        order_later_scales()
        spread_later_scales()
        step(0, 2)
        quantise_x(1, 0, 0, HALF)
        quantise_x(1, 1, 0, HALF)
        step(0, 3)
        product(0, 2)

        block_major = [(b, t) for b in range(BLOCKS) for t in range(PACK)]
        for n in range(1, UNITS):
            g, h = divmod(n, HALVES)
            if h == 0:
                chores = [lambda g=g: order_words(g, 2, both), lambda g=g: order_words(g, 3, both)]
            elif g + 1 < GROUPS:
                chores = [lambda g=g: order_words(g + 1, 0, both), lambda g=g: order_words(g + 1, 1, both)]
            else:
                chores = [lambda: None] * 2
            product(n - 1, 3)
            step(n, 0)
            chores[0]()
            turn_y(n - 1, block_major)
            product(n, 0)
            round_y(n - 1, 0, HALF, nc.vector.tensor_copy)
            chores[1]()
            copy_y(n - 1, 0)
            copy_y(n - 1, 1)
            store_y(n - 1, 0, 2)
            step(n, 1)
            copy_y(n - 1, 2)
            product(n, 1)
            quantise_y(n - 1)
            store_codes(n - 1)
            if n == UNITS - 2:
                store_scales(y_scales_early, 0, GROUPS - 1)
            step(n, 2)
            copy_y(n - 1, 3)
            store_y(n - 1, 2, BLOCKS)
            product(n, 2)
            if n < UNITS - 1:
                step(n, 3)

        n = UNITS - 1
        mid = HALF // 2
        multiply(n, 3)
        sigmoid(n, 3, 0, mid)
        sigmoid(n, 3, mid, HALF)
        product(n, 3, 0, mid)
        product(n, 3, mid, HALF)
        turn_y(n, [(b, t) for b in (0, 1) for t in range(3)] + [(2, 0), (2, 1), (0, 3), (1, 3), (2, 2), (3, 0), (3, 1), (3, 2), (2, 3), (3, 3)])
        round_y(n, 0, mid, nc.vector.tensor_copy)
        round_y(n, mid, HALF, nc.vector.tensor_copy)
        quantise_y(n, 0, HALF)
        for b in range(BLOCKS):
            copy_y(n, b)
            if b == BLOCKS - 1:
                store_codes(n)
            store_y(n, b, b + 1)
        store_scales(y_scales_last, GROUPS - 1, GROUPS)
